import numpy as np
import ml_dtypes


def mxq(x, axis, fmt="e4m3"):
    dtype, down = {"e4m3": (ml_dtypes.float8_e4m3fn, 7), "e5m2": (ml_dtypes.float8_e5m2, 14)}[fmt]
    v = np.moveaxis(np.asarray(x, np.float32).astype(ml_dtypes.bfloat16).astype(np.float64), axis, -1)
    blocks = v.reshape(v.shape[:-1] + (-1, 32))
    amax = np.abs(blocks).max(-1, keepdims=True)
    byte = np.maximum(np.where(amax > 0, np.frexp(amax)[1] - 1 + 127, 0) - down, 1)
    scale = np.exp2(byte - 127.0)
    codes = (blocks / scale).astype(np.float32).astype(dtype).astype(np.float64)
    return np.moveaxis((codes * scale).reshape(v.shape), -1, axis)


WIDE = False


def mx_kscale(k):
    if not WIDE:
        return np.ones(k)
    levels = np.array([10, -10, 5, -5, 0])
    if k % 512:
        return np.exp2(np.random.permutation(np.resize(levels, k // 32))).repeat(32)
    a = np.empty((k // 512, 16))
    for p in range(k // 512):
        a[p, :8] = np.random.permutation(np.resize(levels, 8))
        for g in range(8):
            far = levels[np.abs(levels - a[p, g]) >= 10]
            a[p, g + 8] = far[np.random.randint(len(far))]
    return np.exp2(a.ravel()).repeat(32)


def f64(x):
    return np.asarray(x).astype(np.float64)


def striped8(idx):
    return np.concatenate([x.reshape(-1, 16).T for x in idx]).astype(np.uint16)


def runs(offs, k):
    lists = np.stack([offs[16 * r : 16 * r + 16].T.reshape(-1) for r in range(8)]).astype(np.int64)
    return lists[np.arange(k) % 512 // 64]


def pack_weight(w):
    k, n = w.shape
    w = f64(np.asarray(w, np.float32).astype(ml_dtypes.bfloat16)).reshape(k // 32, 32, n)
    amax = np.abs(w).max(1)
    byte = np.clip(np.where(amax > 0, np.frexp(amax)[1] - 1 + 127 - 7, 1), 1, 254)
    scaled = (w * np.exp2(127.0 - byte)[:, None, :]).reshape(k, n).astype(np.float32)
    words = np.ascontiguousarray(scaled.reshape(k // 512, 128, 4, n).transpose(0, 1, 3, 2)).astype(ml_dtypes.float8_e4m3fn).view(np.uint8)
    return words, np.ascontiguousarray(byte.astype(np.uint8).reshape(k // 512, 16, n))


def unpack_weight(words, scales):
    g, p, n, _ = words.shape
    vals = np.ascontiguousarray(words).view(ml_dtypes.float8_e4m3fn).astype(np.float64) * np.repeat(np.exp2(scales.astype(np.float64) - 127.0), 8, axis=1)[..., None]
    return vals.transpose(0, 1, 3, 2).reshape(g * 512, n)


K, T, S, N, H = 512, 2048, 512, 512, 512


def setup_inputs():
    n = np.random.standard_normal
    s = mx_kscale(K)[:, None]
    u = mx_kscale(H)
    packed_xT = pack_weight(n((K, T)) * s)
    return {
        "x_words": packed_xT[0],
        "x_scales": packed_xT[1],
        "w1": (n((K, H)) / np.sqrt(K) / s).astype(np.float32),
        "w2": (n((K, H)) / np.sqrt(K) / s).astype(np.float32),
        "w3": (n((K, H)) / np.sqrt(K) / s * u).astype(np.float32),
        "w4": (n((H, N)) / np.sqrt(H) / u[:, None]).astype(np.float32),
        "offs": striped8(np.stack([np.random.permutation(T)[:S] for _ in range(8)])),
        "t1": striped8(np.stack([np.random.permutation(S) for _ in range(8)])),
        "t2": striped8(np.stack([np.random.permutation(S) for _ in range(8)])),
    }


def reference(x_words, x_scales, w1, w2, w3, w4, offs, t1, t2):
    xq = unpack_weight(x_words, x_scales)[np.arange(K)[:, None], runs(offs, K)]
    y = mxq(f64(w1), 0, "e4m3").T @ xq
    e = mxq(f64(w2), 0, "e4m3").T @ xq
    val = mxq(f64(w3), 0, "e4m3").T @ xq
    h = e * (val + val[np.arange(H)[:, None], runs(t1, H)])
    z = y * (h + h[np.arange(H)[:, None], runs(t2, H)])
    return mxq(f64(w4), 0, "e4m3").T @ mxq(z, 0, "e4m3")

@@ -1,0 +1,208 @@
+from contextlib import ExitStack
+
+import concourse.mybir as mybir
+
+K, T, S, H, N = 512, 2048, 512, 512, 512
+FLOPS = 2 * S * (3 * K * H + H * N)
+
+F32 = mybir.dt.float32
+BF16 = mybir.dt.bfloat16
+I32 = mybir.dt.int32
+U32 = mybir.dt.uint32
+U16 = mybir.dt.uint16
+U8 = mybir.dt.uint8
+FP8X4 = mybir.dt.float8_e4m3fn_x4
+ADD = mybir.AluOpType.add
+MULT = mybir.AluOpType.mult
+
+P = 128
+PACK = 4
+GROUP = 16
+HALF = S // 2
+CHUNK = 128
+CHUNKS = S // CHUNK
+
+
+def tile_picked_hyena2_none_p_kernel(
+    tc, x_words, x_scales, w1, w2, w3, w4, offs, t1, t2, out
+):
+    nc = tc.nc
+    with ExitStack() as ctx:
+        lists = ctx.enter_context(tc.tile_pool(name="lists", bufs=1))
+        keep = ctx.enter_context(tc.tile_pool(name="keep", bufs=1))
+        psum = ctx.enter_context(tc.psum_pool(name="psum", bufs=1))
+
+        offs_sb = lists.tile([P, S // GROUP], U16, name="offs_sb")
+        t1_sb = lists.tile([P, S // GROUP], U16, name="t1_sb")
+        t2_sb = lists.tile([P, S // GROUP], U16, name="t2_sb")
+
+        def load_weight(w, name, tag):
+            raw = keep.tile([P, PACK, w.shape[1]], F32, name=name, tag=tag)
+            nc.sync.dma_start(out=raw[:], in_=w.rearrange("(p j) n -> p j n", j=PACK))
+            return raw
+
+        scale_table = keep.tile([P, T], U8, name="scale_table")
+        nc.vector.memset(scale_table[:].bitcast(I32), 0)
+        nc.sync.dma_start(out=offs_sb[:], in_=offs)
+        scale_rows = x_scales[0].rearrange("(g r) c -> r g c", r=2)
+        for r in range(2):
+            nc.scalar.dma_start(out=scale_table[r:P:GROUP, :].bitcast(I32), in_=scale_rows[r].bitcast(I32))
+        word_table = keep.tile([P, T], U32, name="word_table", tag="early_a")
+        nc.sync.dma_start(
+            out=word_table[:].bitcast(I32), in_=x_words[0].rearrange("p c r -> p (c r)").bitcast(I32)
+        )
+        w3_raw = load_weight(w3, "w3_raw", "early_b")
+        nc.sync.dma_start(out=t1_sb[:], in_=t1)
+        w2_raw = load_weight(w2, "w2_raw", "w2_raw")
+        nc.sync.dma_start(out=t2_sb[:], in_=t2)
+
+        picked_scales = keep.tile([P, S], U8, name="picked_scales")
+        nc.vector.tensor_copy(picked_scales[:], scale_table[:].indirect(offs_sb[:]))
+        x_scale = keep.tile([P, S], U8, name="x_scale", align_bytes=64)
+        nc.vector.tensor_copy(x_scale[:].bitcast(I32), picked_scales[:].bitcast(I32))
+        for r in range(2):
+            nc.scalar.dma_start(
+                out=x_scale[2 + r : P : 32, :].bitcast(I32), in_=picked_scales[GROUP + r : P : 32, :].bitcast(I32)
+            )
+        x_codes = keep.tile([P, S], U32, name="x_codes", align_bytes=64)
+        nc.vector.tensor_copy(x_codes[:], word_table[:].indirect(offs_sb[:]))
+
+        def mx_tiles(name, width):
+            codes = keep.tile([P, width], U32, name=name + "_codes", align_bytes=64)
+            scales = keep.tile([P, width], U8, name=name + "_scales", align_bytes=64)
+            return codes, scales
+
+        def cast_pair(copy, raw, pair, name):
+            grouped = keep.tile([P, 2 * P * PACK], BF16, name="%s_pair%d" % (name, pair), align_bytes=64)
+            src = raw[:].rearrange("p j (m u t) -> p u m j t", u=2, t=2)[:, pair]
+            copy(out=grouped[:].rearrange("p (t m j) -> p m j t", t=2, j=PACK), in_=src)
+            return grouped
+
+        def quantize(mx, first, grouped_ap):
+            codes, scales = mx
+            cols = slice(first, first + grouped_ap.shape[1] // PACK)
+            nc.vector.quantize_mx(out=codes[:, cols].bitcast(FP8X4), scales=scales[:, cols], in_=grouped_ap)
+
+        def product(acc, weights, w_cols, moving, m_cols):
+            nc.tensor.matmul_mx(
+                out=acc,
+                lhsT=weights[0][:, w_cols].bitcast(FP8X4),
+                lhsT_scale=weights[1][:, w_cols],
+                rhs=moving[0][:, m_cols].bitcast(FP8X4),
+                rhs_scale=moving[1][:, m_cols],
+                start=True,
+                stop=True,
+            )
+
+        x_mx = (x_codes, x_scale)
+        w1_mx, w2_mx, w3_mx, w4_mx = [mx_tiles(name, H) for name in ("w1", "w2", "w3", "w4")]
+        everything = slice(0, S)
+
+        def plane_cols(t):
+            return slice(t * P, (t + 1) * P)
+
+        def list_cols(first, count):
+            return slice(first // GROUP, (first + count) // GROUP)
+
+        w3_front = cast_pair(nc.vector.tensor_copy, w3_raw, 0, "w3")
+        w3_back = cast_pair(nc.scalar.copy, w3_raw, 1, "w3")
+        quantize(w3_mx, 0, w3_front[:, : P * PACK])
+        quantize(w3_mx, P, w3_front[:, P * PACK :])
+        quantize(w3_mx, 2 * P, w3_back[:])
+        w1_raw = load_weight(w1, "w1_raw", "early_a")
+        w4_raw = load_weight(w4, "w4_raw", "early_b")
+
+        last = PACK - 1
+        val_tile = [keep.tile([P, S if t == 0 else 2 * S], F32, name="val_tile%d" % t) for t in range(PACK)]
+        val_plain = [val_tile[t + 1][:, S:] for t in range(last)] + [keep.tile([P, S], F32, name="val_plain")[:]]
+        h_tile = [keep.tile([P, S if t == last else 2 * S], F32, name="h_tile%d" % t) for t in range(PACK)]
+        val_sum = [h_tile[t][:, S:] for t in range(last)] + [keep.tile([P, S], F32, name="val_sum")[:]]
+        h_plain = [keep.tile([P, S], F32, name="h_plain%d" % t) for t in range(PACK)]
+        h_sum = keep.tile([P, PACK, S], F32, name="h_sum")
+
+        def tap(total, window, offsets, plain, first, count):
+            cols = slice(first, first + count)
+            nc.vector.tensor_tensor(
+                total[:, cols], window[:].indirect(offsets[:, list_cols(first, count)]), plain[:, cols], ADD
+            )
+
+        def first_tap(t):
+            val = psum.tile([P, S], F32, name="val", tag="val_out", bufs=2)
+            product(val[:], w3_mx, plane_cols(t), x_mx, everything)
+            nc.scalar.copy(out=val_tile[t][:, :S], in_=val[:])
+            if t == 0:
+                nc.vector.tensor_copy(out=val_plain[t], in_=val[:])
+                for first in (0, HALF):
+                    tap(val_sum[t], val_tile[t], t1_sb, val_plain[t], first, HALF)
+            else:
+                nc.scalar.copy(out=val_plain[t], in_=val[:])
+                tap(val_sum[t], val_tile[t], t1_sb, val_plain[t], 0, S)
+
+        def first_gate(t):
+            e = psum.tile([P, S], F32, name="e", tag="e_out", bufs=2)
+            product(e[:], w2_mx, plane_cols(t), x_mx, everything)
+            nc.vector.tensor_tensor(h_tile[t][:, :S], val_sum[t], e[:], MULT)
+            nc.sync.dma_start(out=h_plain[t][:], in_=h_tile[t][:, :S])
+
+        def second_tap(t, first, count):
+            tap(h_sum[:, t, :], h_tile[t], t2_sb, h_plain[t][:], first, count)
+
+        first_tap(0)
+        first_tap(1)
+        quantize(w2_mx, 0, cast_pair(nc.scalar.copy, w2_raw, 0, "w2")[:])
+        first_tap(2)
+        first_gate(0)
+        first_tap(3)
+        first_gate(1)
+        quantize(w2_mx, 2 * P, cast_pair(nc.scalar.copy, w2_raw, 1, "w2")[:])
+        first_gate(2)
+        first_gate(3)
+
+        for pair in range(2):
+            quantize(w1_mx, 2 * P * pair, cast_pair(nc.scalar.copy, w1_raw, pair, "w1")[:])
+        second_tap(0, 0, S)
+        y = []
+        for c in range(CHUNKS):
+            bank = psum.tile([P, PACK, CHUNK], F32, name="y%d" % c)
+            for t in range(PACK):
+                product(bank[:, t, :], w1_mx, plane_cols(t), x_mx, slice(c * CHUNK, (c + 1) * CHUNK))
+            y.append(bank)
+        w4_grouped = keep.tile([P, N * PACK], BF16, name="w4_grouped", align_bytes=64)
+        nc.scalar.copy(
+            out=w4_grouped[:].rearrange("p (c i j) -> p c j i", i=4, j=PACK),
+            in_=w4_raw[:].rearrange("p j (c i) -> p c j i", i=4),
+        )
+        second_tap(1, 0, S)
+        quantize(w4_mx, 0, w4_grouped[:])
+        second_tap(2, 0, S)
+
+        out_rows = out.rearrange("(a p) s -> p a s", p=P)
+        z_grouped = {}
+
+        def second_gate(c):
+            cols = slice(c * CHUNK, (c + 1) * CHUNK)
+            z_grouped[c] = keep.tile([P, CHUNK * PACK], BF16, name="z_grouped%d" % c, align_bytes=64)
+            nc.vector.tensor_tensor(
+                z_grouped[c][:].rearrange("p (c i t) -> p c t i", i=2, t=PACK),
+                h_sum[:, :, cols].rearrange("p t (c i) -> p c t i", i=2),
+                y[c][:].rearrange("p t (c i) -> p c t i", i=2),
+                MULT,
+            )
+
+        def last_layer(c):
+            z_mx = mx_tiles("z%d" % c, CHUNK)
+            quantize(z_mx, 0, z_grouped[c][:])
+            acc = psum.tile([P, N // P, CHUNK], F32, name="acc", tag=("val_out", "e_out")[c % 2], bufs=2)
+            for a in range(N // P):
+                product(acc[:, a, :], w4_mx, plane_cols(a), z_mx, slice(0, CHUNK))
+            result = keep.tile([P, N // P, CHUNK], F32, name="result%d" % c)
+            nc.scalar.copy(out=result[:], in_=acc[:])
+            nc.sync.dma_start(out=out_rows[:, :, c * CHUNK : (c + 1) * CHUNK], in_=result[:])
+
+        for step in range(CHUNKS + 2):
+            if step < CHUNKS:
+                second_tap(PACK - 1, step * CHUNK, CHUNK)
+            if 1 <= step <= CHUNKS:
+                second_gate(step - 1)
+            if step >= 2:
+                last_layer(step - 2)

@@ -41,41 +41,42 @@ def tile_picked_hyena2_none_p_kernel(
             nc.sync.dma_start(out=raw[:], in_=w.rearrange("(p j) n -> p j n", j=PACK))
             return raw
 
-        scale_table = keep.tile([P, T], U8, name="scale_table")
+        scale_table = keep.tile([P, T], U8, name="scale_table", tag="slot_a")
         nc.vector.memset(scale_table[:].bitcast(I32), 0)
+        x_scale = keep.tile([P, S], U8, name="x_scale", align_bytes=64)
+        nc.vector.memset(x_scale[:].bitcast(I32), 0)
         nc.sync.dma_start(out=offs_sb[:], in_=offs)
-        scale_rows = x_scales[0].rearrange("(g r) c -> r g c", r=2)
-        for r in range(2):
-            nc.scalar.dma_start(out=scale_table[r:P:GROUP, :].bitcast(I32), in_=scale_rows[r].bitcast(I32))
-        word_table = keep.tile([P, T], U32, name="word_table", tag="early_a")
+        w3_raw = keep.tile([P, PACK, H], F32, name="w3_raw")
+        w3_rows = w3.rearrange("(p j) n -> p j n", j=PACK)
+        nc.sync.dma_start(out=w3_raw[:, :1, :], in_=w3_rows[:, :1, :])
+        nc.sync.dma_start(out=t1_sb[:], in_=t1)
+        nc.sync.dma_start(out=t2_sb[:], in_=t2)
+        nc.sync.dma_start(out=scale_table[0:P:8, :].bitcast(I32), in_=x_scales[0].bitcast(I32))
+        nc.sync.dma_start(out=w3_raw[:, 1:, :], in_=w3_rows[:, 1:, :])
+        word_table = keep.tile([P, T], U32, name="word_table", tag="slot_b")
         nc.sync.dma_start(
             out=word_table[:].bitcast(I32), in_=x_words[0].rearrange("p c r -> p (c r)").bitcast(I32)
         )
-        w3_raw = load_weight(w3, "w3_raw", "early_b")
-        nc.sync.dma_start(out=t1_sb[:], in_=t1)
-        w2_raw = load_weight(w2, "w2_raw", "w2_raw")
-        nc.sync.dma_start(out=t2_sb[:], in_=t2)
 
-        picked_scales = keep.tile([P, S], U8, name="picked_scales")
+        picked_scales = keep.tile([P, S], U8, name="picked_scales", tag="slot_c")
         nc.vector.tensor_copy(picked_scales[:], scale_table[:].indirect(offs_sb[:]))
-        x_scale = keep.tile([P, S], U8, name="x_scale", align_bytes=64)
-        nc.vector.tensor_copy(x_scale[:].bitcast(I32), picked_scales[:].bitcast(I32))
-        for r in range(2):
-            nc.scalar.dma_start(
-                out=x_scale[2 + r : P : 32, :].bitcast(I32), in_=picked_scales[GROUP + r : P : 32, :].bitcast(I32)
-            )
-        x_codes = keep.tile([P, S], U32, name="x_codes", align_bytes=64)
-        nc.vector.tensor_copy(x_codes[:], word_table[:].indirect(offs_sb[:]))
+        for j in range(4):
+            (nc.sync, nc.scalar)[j % 2].dma_start(out=x_scale[j:P:32, :].bitcast(I32), in_=picked_scales[8 * j : P : 32, :].bitcast(I32))
+        w2_raw = load_weight(w2, "w2_raw", "slot_a")
+        w1_raw = load_weight(w1, "w1_raw", "slot_c")
 
         def mx_tiles(name, width):
             codes = keep.tile([P, width], U32, name=name + "_codes", align_bytes=64)
             scales = keep.tile([P, width], U8, name=name + "_scales", align_bytes=64)
             return codes, scales
 
-        def cast_pair(copy, raw, pair, name):
+        def cast_pair(shares, raw, pair, name):
             grouped = keep.tile([P, 2 * P * PACK], BF16, name="%s_pair%d" % (name, pair), align_bytes=64)
             src = raw[:].rearrange("p j (m u t) -> p u m j t", u=2, t=2)[:, pair]
-            copy(out=grouped[:].rearrange("p (t m j) -> p m j t", t=2, j=PACK), in_=src)
+            dst = grouped[:].rearrange("p (t m j) -> p m j t", t=2, j=PACK)
+            width = P // len(shares)
+            for i, copy in enumerate(shares):
+                copy(out=dst[:, i * width : (i + 1) * width], in_=src[:, i * width : (i + 1) * width])
             return grouped
 
         def quantize(mx, first, grouped_ap):
@@ -94,7 +95,6 @@ def tile_picked_hyena2_none_p_kernel(
                 stop=True,
             )
 
-        x_mx = (x_codes, x_scale)
         w1_mx, w2_mx, w3_mx, w4_mx = [mx_tiles(name, H) for name in ("w1", "w2", "w3", "w4")]
         everything = slice(0, S)
 
@@ -104,13 +104,17 @@ def tile_picked_hyena2_none_p_kernel(
         def list_cols(first, count):
             return slice(first // GROUP, (first + count) // GROUP)
 
-        w3_front = cast_pair(nc.vector.tensor_copy, w3_raw, 0, "w3")
-        w3_back = cast_pair(nc.scalar.copy, w3_raw, 1, "w3")
-        quantize(w3_mx, 0, w3_front[:, : P * PACK])
-        quantize(w3_mx, P, w3_front[:, P * PACK :])
+        w3_front = cast_pair([nc.vector.tensor_copy], w3_raw, 0, "w3")
+        w3_back = cast_pair([nc.vector.tensor_copy, nc.scalar.copy], w3_raw, 1, "w3")
+        quantize(w3_mx, 0, w3_front[:])
         quantize(w3_mx, 2 * P, w3_back[:])
-        w1_raw = load_weight(w1, "w1_raw", "early_a")
-        w4_raw = load_weight(w4, "w4_raw", "early_b")
+        x_codes = keep.tile([P, S], U32, name="x_codes", align_bytes=64)
+        for first in (0, HALF):
+            nc.vector.tensor_copy(
+                x_codes[:, first : first + HALF], word_table[:].indirect(offs_sb[:, list_cols(first, HALF)])
+            )
+        x_mx = (x_codes, x_scale)
+        w4_raw = load_weight(w4, "w4_raw", "slot_b")
 
         last = PACK - 1
         val_tile = [keep.tile([P, S if t == 0 else 2 * S], F32, name="val_tile%d" % t) for t in range(PACK)]
@@ -127,14 +131,22 @@ def tile_picked_hyena2_none_p_kernel(
             )
 
         def first_tap(t):
-            val = psum.tile([P, S], F32, name="val", tag="val_out", bufs=2)
-            product(val[:], w3_mx, plane_cols(t), x_mx, everything)
-            nc.scalar.copy(out=val_tile[t][:, :S], in_=val[:])
             if t == 0:
-                nc.vector.tensor_copy(out=val_plain[t], in_=val[:])
+                halves = []
+                for first in (0, HALF):
+                    cols = slice(first, first + HALF)
+                    val = psum.tile([P, HALF], F32, name="val_half", tag="y%d" % (first // HALF))
+                    product(val[:], w3_mx, plane_cols(t), x_mx, cols)
+                    nc.scalar.copy(out=val_tile[t][:, cols], in_=val[:])
+                    halves.append(val)
+                for first in (0, HALF):
+                    nc.vector.tensor_copy(out=val_plain[t][:, first : first + HALF], in_=halves[first // HALF][:])
                 for first in (0, HALF):
                     tap(val_sum[t], val_tile[t], t1_sb, val_plain[t], first, HALF)
             else:
+                val = psum.tile([P, S], F32, name="val", tag="val_out", bufs=2)
+                product(val[:], w3_mx, plane_cols(t), x_mx, everything)
+                nc.scalar.copy(out=val_tile[t][:, :S], in_=val[:])
                 nc.scalar.copy(out=val_plain[t], in_=val[:])
                 tap(val_sum[t], val_tile[t], t1_sb, val_plain[t], 0, S)
 
@@ -149,21 +161,21 @@ def tile_picked_hyena2_none_p_kernel(
 
         first_tap(0)
         first_tap(1)
-        quantize(w2_mx, 0, cast_pair(nc.scalar.copy, w2_raw, 0, "w2")[:])
+        quantize(w2_mx, 0, cast_pair([nc.scalar.copy], w2_raw, 0, "w2")[:])
         first_tap(2)
         first_gate(0)
-        first_tap(3)
         first_gate(1)
-        quantize(w2_mx, 2 * P, cast_pair(nc.scalar.copy, w2_raw, 1, "w2")[:])
+        first_tap(3)
+        quantize(w2_mx, 2 * P, cast_pair([nc.scalar.copy], w2_raw, 1, "w2")[:])
         first_gate(2)
         first_gate(3)
 
         for pair in range(2):
-            quantize(w1_mx, 2 * P * pair, cast_pair(nc.scalar.copy, w1_raw, pair, "w1")[:])
+            quantize(w1_mx, 2 * P * pair, cast_pair([nc.scalar.copy], w1_raw, pair, "w1")[:])
         second_tap(0, 0, S)
         y = []
         for c in range(CHUNKS):
-            bank = psum.tile([P, PACK, CHUNK], F32, name="y%d" % c)
+            bank = psum.tile([P, PACK, CHUNK], F32, name="y%d" % c, tag="y%d" % c)
             for t in range(PACK):
                 product(bank[:, t, :], w1_mx, plane_cols(t), x_mx, slice(c * CHUNK, (c + 1) * CHUNK))
             y.append(bank)
@@ -192,12 +204,18 @@ def tile_picked_hyena2_none_p_kernel(
         def last_layer(c):
             z_mx = mx_tiles("z%d" % c, CHUNK)
             quantize(z_mx, 0, z_grouped[c][:])
-            acc = psum.tile([P, N // P, CHUNK], F32, name="acc", tag=("val_out", "e_out")[c % 2], bufs=2)
-            for a in range(N // P):
-                product(acc[:, a, :], w4_mx, plane_cols(a), z_mx, slice(0, CHUNK))
-            result = keep.tile([P, N // P, CHUNK], F32, name="result%d" % c)
-            nc.scalar.copy(out=result[:], in_=acc[:])
-            nc.sync.dma_start(out=out_rows[:, :, c * CHUNK : (c + 1) * CHUNK], in_=result[:])
+            cols = slice(c * CHUNK, (c + 1) * CHUNK)
+            if c < CHUNKS - 1:
+                parts = [(0, N // P, nc.scalar.copy, nc.sync, ("val_out", "e_out")[c % 2])]
+            else:
+                parts = [(0, 2, nc.scalar.copy, nc.scalar, "e_out"), (2, 2, nc.vector.tensor_copy, nc.sync, "val_out")]
+            for first, count, copy, queue, tag in parts:
+                acc = psum.tile([P, count, CHUNK], F32, name="acc", tag=tag, bufs=2)
+                for a in range(count):
+                    product(acc[:, a, :], w4_mx, plane_cols(first + a), z_mx, slice(0, CHUNK))
+                result = keep.tile([P, count, CHUNK], F32, name="result%d_%d" % (c, first))
+                copy(out=result[:], in_=acc[:])
+                queue.dma_start(out=out_rows[:, first : first + count, cols], in_=result[:])
 
         for step in range(CHUNKS + 2):
             if step < CHUNKS:

@@ -41,6 +41,10 @@ def tile_picked_hyena2_none_p_kernel(
             nc.sync.dma_start(out=raw[:], in_=w.rearrange("(p j) n -> p j n", j=PACK))
             return raw
 
+        warm_in = keep.tile([P, 1], F32, name="warm_in")
+        warm_out = keep.tile([P, 1], BF16, name="warm_out")
+        nc.gpsimd.memset(warm_in[:], 0.0)
+        nc.scalar.copy(out=warm_out[:], in_=warm_in[:])
         scale_table = keep.tile([P, T], U8, name="scale_table", tag="slot_a")
         nc.vector.memset(scale_table[:].bitcast(I32), 0)
         x_scale = keep.tile([P, S], U8, name="x_scale", align_bytes=64)
@@ -61,7 +65,7 @@ def tile_picked_hyena2_none_p_kernel(
         picked_scales = keep.tile([P, S], U8, name="picked_scales", tag="slot_c")
         nc.vector.tensor_copy(picked_scales[:], scale_table[:].indirect(offs_sb[:]))
         for j in range(4):
-            (nc.sync, nc.scalar)[j % 2].dma_start(out=x_scale[j:P:32, :].bitcast(I32), in_=picked_scales[8 * j : P : 32, :].bitcast(I32))
+            nc.sync.dma_start(out=x_scale[j:P:32, :].bitcast(I32), in_=picked_scales[8 * j : P : 32, :].bitcast(I32))
         w2_raw = load_weight(w2, "w2_raw", "slot_a")
         w1_raw = load_weight(w1, "w1_raw", "slot_c")
 
@@ -105,7 +109,7 @@ def tile_picked_hyena2_none_p_kernel(
             return slice(first // GROUP, (first + count) // GROUP)
 
         w3_front = cast_pair([nc.vector.tensor_copy], w3_raw, 0, "w3")
-        w3_back = cast_pair([nc.vector.tensor_copy, nc.scalar.copy], w3_raw, 1, "w3")
+        w3_back = cast_pair([nc.scalar.copy], w3_raw, 1, "w3")
         quantize(w3_mx, 0, w3_front[:])
         quantize(w3_mx, 2 * P, w3_back[:])
         x_codes = keep.tile([P, S], U32, name="x_codes", align_bytes=64)
@@ -130,49 +134,64 @@ def tile_picked_hyena2_none_p_kernel(
                 total[:, cols], window[:].indirect(offsets[:, list_cols(first, count)]), plain[:, cols], ADD
             )
 
-        def first_tap(t):
+        def project_val(t):
             if t == 0:
-                halves = []
                 for first in (0, HALF):
                     cols = slice(first, first + HALF)
                     val = psum.tile([P, HALF], F32, name="val_half", tag="y%d" % (first // HALF))
                     product(val[:], w3_mx, plane_cols(t), x_mx, cols)
                     nc.scalar.copy(out=val_tile[t][:, cols], in_=val[:])
-                    halves.append(val)
-                for first in (0, HALF):
-                    nc.vector.tensor_copy(out=val_plain[t][:, first : first + HALF], in_=halves[first // HALF][:])
-                for first in (0, HALF):
-                    tap(val_sum[t], val_tile[t], t1_sb, val_plain[t], first, HALF)
+                    (nc.scalar.copy if first else nc.vector.tensor_copy)(out=val_plain[t][:, cols], in_=val[:])
             else:
                 val = psum.tile([P, S], F32, name="val", tag="val_out", bufs=2)
                 product(val[:], w3_mx, plane_cols(t), x_mx, everything)
                 nc.scalar.copy(out=val_tile[t][:, :S], in_=val[:])
                 nc.scalar.copy(out=val_plain[t], in_=val[:])
-                tap(val_sum[t], val_tile[t], t1_sb, val_plain[t], 0, S)
+
+        def first_tap(t):
+            count = HALF if t == 0 else S
+            for first in range(0, S, count):
+                tap(val_sum[t], val_tile[t], t1_sb, val_plain[t], first, count)
 
         def first_gate(t):
             e = psum.tile([P, S], F32, name="e", tag="e_out", bufs=2)
             product(e[:], w2_mx, plane_cols(t), x_mx, everything)
             nc.vector.tensor_tensor(h_tile[t][:, :S], val_sum[t], e[:], MULT)
-            nc.sync.dma_start(out=h_plain[t][:], in_=h_tile[t][:, :S])
+
+        def copy_h(t, first, count):
+            cols = slice(first, first + count)
+            nc.scalar.copy(out=h_plain[t][:, cols], in_=h_tile[t][:, cols])
 
         def second_tap(t, first, count):
             tap(h_sum[:, t, :], h_tile[t], t2_sb, h_plain[t][:], first, count)
 
+        project_val(0)
+        project_val(1)
+        w2_front = cast_pair([nc.vector.tensor_copy, nc.scalar.copy], w2_raw, 0, "w2")
         first_tap(0)
         first_tap(1)
-        quantize(w2_mx, 0, cast_pair([nc.scalar.copy], w2_raw, 0, "w2")[:])
-        first_tap(2)
+        quantize(w2_mx, 0, w2_front[:])
+        for t in (2, 3):
+            project_val(t)
+            first_tap(t)
+        w2_back = cast_pair([nc.scalar.copy], w2_raw, 1, "w2")
         first_gate(0)
+        copy_h(0, 0, S)
         first_gate(1)
-        first_tap(3)
-        quantize(w2_mx, 2 * P, cast_pair([nc.scalar.copy], w2_raw, 1, "w2")[:])
+        copy_h(1, 0, S)
+        quantize(w2_mx, 2 * P, w2_back[:])
+        second_tap(0, 0, S)
         first_gate(2)
         first_gate(3)
-
+        w1_grouped = keep.tile([P, H * PACK], BF16, name="w1_grouped", align_bytes=64)
         for pair in range(2):
-            quantize(w1_mx, 2 * P * pair, cast_pair([nc.scalar.copy], w1_raw, pair, "w1")[:])
-        second_tap(0, 0, S)
+            nc.scalar.copy(
+                out=w1_grouped[:].rearrange("p (u t m j) -> p u m j t", u=2, t=2, j=PACK)[:, pair],
+                in_=w1_raw[:].rearrange("p j (m u t) -> p u m j t", u=2, t=2)[:, pair],
+            )
+        second_tap(1, 0, S)
+        quantize(w1_mx, 0, w1_grouped[:])
+        copy_h(2, 0, S)
         y = []
         for c in range(CHUNKS):
             bank = psum.tile([P, PACK, CHUNK], F32, name="y%d" % c, tag="y%d" % c)
@@ -184,9 +203,10 @@ def tile_picked_hyena2_none_p_kernel(
             out=w4_grouped[:].rearrange("p (c i j) -> p c j i", i=4, j=PACK),
             in_=w4_raw[:].rearrange("p j (c i) -> p c j i", i=4),
         )
-        second_tap(1, 0, S)
-        quantize(w4_mx, 0, w4_grouped[:])
         second_tap(2, 0, S)
+        quantize(w4_mx, 0, w4_grouped[:])
+        for first in (0, HALF):
+            copy_h(last, first, HALF)
 
         out_rows = out.rearrange("(a p) s -> p a s", p=P)
         z_grouped = {}
@@ -205,22 +225,23 @@ def tile_picked_hyena2_none_p_kernel(
             z_mx = mx_tiles("z%d" % c, CHUNK)
             quantize(z_mx, 0, z_grouped[c][:])
             cols = slice(c * CHUNK, (c + 1) * CHUNK)
-            if c < CHUNKS - 1:
-                parts = [(0, N // P, nc.scalar.copy, nc.sync, ("val_out", "e_out")[c % 2])]
+            if c < 2:
+                parts = [(0, N // P, nc.scalar.copy, nc.sync)]
             else:
-                parts = [(0, 2, nc.scalar.copy, nc.scalar, "e_out"), (2, 2, nc.vector.tensor_copy, nc.sync, "val_out")]
-            for first, count, copy, queue, tag in parts:
-                acc = psum.tile([P, count, CHUNK], F32, name="acc", tag=tag, bufs=2)
+                parts = [(0, 2, nc.scalar.copy, nc.scalar), (2, 2, nc.vector.tensor_copy, nc.sync)]
+            for first, count, copy, queue in parts:
+                acc = psum.tile([P, count, CHUNK], F32, name="acc", tag=("val_out", "e_out")[(c + first // 2) % 2], bufs=2)
                 for a in range(count):
                     product(acc[:, a, :], w4_mx, plane_cols(first + a), z_mx, slice(0, CHUNK))
                 result = keep.tile([P, count, CHUNK], F32, name="result%d_%d" % (c, first))
                 copy(out=result[:], in_=acc[:])
                 queue.dma_start(out=out_rows[:, first : first + count, cols], in_=result[:])
 
-        for step in range(CHUNKS + 2):
-            if step < CHUNKS:
-                second_tap(PACK - 1, step * CHUNK, CHUNK)
-            if 1 <= step <= CHUNKS:
-                second_gate(step - 1)
-            if step >= 2:
-                last_layer(step - 2)
+        second_tap(last, 0, HALF)
+        for c in range(CHUNKS):
+            if c < 2:
+                second_tap(last, HALF + c * CHUNK, CHUNK)
+            second_gate(c)
+            if c >= 1:
+                last_layer(c - 1)
+        last_layer(CHUNKS - 1)

from contextlib import ExitStack

import concourse.mybir as mybir

K, T, S, H, N = 512, 2048, 512, 512, 512
FLOPS = 2 * S * (3 * K * H + H * N)

F32 = mybir.dt.float32
BF16 = mybir.dt.bfloat16
I32 = mybir.dt.int32
U32 = mybir.dt.uint32
U16 = mybir.dt.uint16
U8 = mybir.dt.uint8
FP8X4 = mybir.dt.float8_e4m3fn_x4
ADD = mybir.AluOpType.add
MULT = mybir.AluOpType.mult

P = 128
PACK = 4
GROUP = 16
HALF = S // 2
CHUNK = 128
CHUNKS = S // CHUNK


def tile_picked_hyena2_none_p_kernel(
    tc, x_words, x_scales, w1, w2, w3, w4, offs, t1, t2, out
):
    nc = tc.nc
    with ExitStack() as ctx:
        lists = ctx.enter_context(tc.tile_pool(name="lists", bufs=1))
        keep = ctx.enter_context(tc.tile_pool(name="keep", bufs=1))
        psum = ctx.enter_context(tc.psum_pool(name="psum", bufs=1))

        offs_sb = lists.tile([P, S // GROUP], U16, name="offs_sb")
        t1_sb = lists.tile([P, S // GROUP], U16, name="t1_sb")
        t2_sb = lists.tile([P, S // GROUP], U16, name="t2_sb")

        def load_weight(w, name, tag):
            raw = keep.tile([P, PACK, w.shape[1]], F32, name=name, tag=tag)
            nc.sync.dma_start(out=raw[:], in_=w.rearrange("(p j) n -> p j n", j=PACK))
            return raw

        warm_in = keep.tile([P, 1], F32, name="warm_in")
        warm_out = keep.tile([P, 1], BF16, name="warm_out")
        nc.gpsimd.memset(warm_in[:], 0.0)
        nc.scalar.copy(out=warm_out[:], in_=warm_in[:])
        scale_table = keep.tile([P, T], U8, name="scale_table", tag="slot_a")
        nc.vector.memset(scale_table[:].bitcast(I32), 0)
        x_scale = keep.tile([P, S], U8, name="x_scale", align_bytes=64)
        nc.vector.memset(x_scale[:].bitcast(I32), 0)
        nc.sync.dma_start(out=offs_sb[:], in_=offs)
        w3_raw = keep.tile([P, PACK, H], F32, name="w3_raw")
        w3_rows = w3.rearrange("(p j) n -> p j n", j=PACK)
        nc.sync.dma_start(out=w3_raw[:, :1, :], in_=w3_rows[:, :1, :])
        nc.sync.dma_start(out=t1_sb[:], in_=t1)
        nc.sync.dma_start(out=t2_sb[:], in_=t2)
        nc.sync.dma_start(out=scale_table[0:P:8, :].bitcast(I32), in_=x_scales[0].bitcast(I32))
        nc.sync.dma_start(out=w3_raw[:, 1:, :], in_=w3_rows[:, 1:, :])
        word_table = keep.tile([P, T], U32, name="word_table", tag="slot_b")
        nc.sync.dma_start(
            out=word_table[:].bitcast(I32), in_=x_words[0].rearrange("p c r -> p (c r)").bitcast(I32)
        )

        picked_scales = keep.tile([P, S], U8, name="picked_scales", tag="slot_c")
        nc.vector.tensor_copy(picked_scales[:], scale_table[:].indirect(offs_sb[:]))
        for j in range(4):
            nc.sync.dma_start(out=x_scale[j:P:32, :].bitcast(I32), in_=picked_scales[8 * j : P : 32, :].bitcast(I32))
        w2_raw = load_weight(w2, "w2_raw", "slot_a")
        w1_raw = load_weight(w1, "w1_raw", "slot_c")

        def mx_tiles(name, width):
            codes = keep.tile([P, width], U32, name=name + "_codes", align_bytes=64)
            scales = keep.tile([P, width], U8, name=name + "_scales", align_bytes=64)
            return codes, scales

        def cast_pair(shares, raw, pair, name):
            grouped = keep.tile([P, 2 * P * PACK], BF16, name="%s_pair%d" % (name, pair), align_bytes=64)
            src = raw[:].rearrange("p j (m u t) -> p u m j t", u=2, t=2)[:, pair]
            dst = grouped[:].rearrange("p (t m j) -> p m j t", t=2, j=PACK)
            width = P // len(shares)
            for i, copy in enumerate(shares):
                copy(out=dst[:, i * width : (i + 1) * width], in_=src[:, i * width : (i + 1) * width])
            return grouped

        def quantize(mx, first, grouped_ap):
            codes, scales = mx
            cols = slice(first, first + grouped_ap.shape[1] // PACK)
            nc.vector.quantize_mx(out=codes[:, cols].bitcast(FP8X4), scales=scales[:, cols], in_=grouped_ap)

        def product(acc, weights, w_cols, moving, m_cols):
            nc.tensor.matmul_mx(
                out=acc,
                lhsT=weights[0][:, w_cols].bitcast(FP8X4),
                lhsT_scale=weights[1][:, w_cols],
                rhs=moving[0][:, m_cols].bitcast(FP8X4),
                rhs_scale=moving[1][:, m_cols],
                start=True,
                stop=True,
            )

        w1_mx, w2_mx, w3_mx, w4_mx = [mx_tiles(name, H) for name in ("w1", "w2", "w3", "w4")]
        everything = slice(0, S)

        def plane_cols(t):
            return slice(t * P, (t + 1) * P)

        def list_cols(first, count):
            return slice(first // GROUP, (first + count) // GROUP)

        w3_front = cast_pair([nc.vector.tensor_copy], w3_raw, 0, "w3")
        w3_back = cast_pair([nc.scalar.copy], w3_raw, 1, "w3")
        quantize(w3_mx, 0, w3_front[:])
        quantize(w3_mx, 2 * P, w3_back[:])
        x_codes = keep.tile([P, S], U32, name="x_codes", align_bytes=64)
        for first in (0, HALF):
            nc.vector.tensor_copy(
                x_codes[:, first : first + HALF], word_table[:].indirect(offs_sb[:, list_cols(first, HALF)])
            )
        x_mx = (x_codes, x_scale)
        w4_raw = load_weight(w4, "w4_raw", "slot_b")

        last = PACK - 1
        val_tile = [keep.tile([P, S if t == 0 else 2 * S], F32, name="val_tile%d" % t) for t in range(PACK)]
        val_plain = [val_tile[t + 1][:, S:] for t in range(last)] + [keep.tile([P, S], F32, name="val_plain")[:]]
        h_tile = [keep.tile([P, S if t == last else 2 * S], F32, name="h_tile%d" % t) for t in range(PACK)]
        val_sum = [h_tile[t][:, S:] for t in range(last)] + [keep.tile([P, S], F32, name="val_sum")[:]]
        h_plain = [keep.tile([P, S], F32, name="h_plain%d" % t) for t in range(PACK)]
        h_sum = keep.tile([P, PACK, S], F32, name="h_sum")

        def tap(total, window, offsets, plain, first, count):
            cols = slice(first, first + count)
            nc.vector.tensor_tensor(
                total[:, cols], window[:].indirect(offsets[:, list_cols(first, count)]), plain[:, cols], ADD
            )

        def project_val(t):
            if t == 0:
                for first in (0, HALF):
                    cols = slice(first, first + HALF)
                    val = psum.tile([P, HALF], F32, name="val_half", tag="y%d" % (first // HALF))
                    product(val[:], w3_mx, plane_cols(t), x_mx, cols)
                    nc.scalar.copy(out=val_tile[t][:, cols], in_=val[:])
                    (nc.scalar.copy if first else nc.vector.tensor_copy)(out=val_plain[t][:, cols], in_=val[:])
            else:
                val = psum.tile([P, S], F32, name="val", tag="val_out", bufs=2)
                product(val[:], w3_mx, plane_cols(t), x_mx, everything)
                nc.scalar.copy(out=val_tile[t][:, :S], in_=val[:])
                nc.scalar.copy(out=val_plain[t], in_=val[:])

        def first_tap(t):
            count = HALF if t == 0 else S
            for first in range(0, S, count):
                tap(val_sum[t], val_tile[t], t1_sb, val_plain[t], first, count)

        def first_gate(t):
            e = psum.tile([P, S], F32, name="e", tag="e_out", bufs=2)
            product(e[:], w2_mx, plane_cols(t), x_mx, everything)
            nc.vector.tensor_tensor(h_tile[t][:, :S], val_sum[t], e[:], MULT)

        def copy_h(t, first, count):
            cols = slice(first, first + count)
            nc.scalar.copy(out=h_plain[t][:, cols], in_=h_tile[t][:, cols])

        def second_tap(t, first, count):
            tap(h_sum[:, t, :], h_tile[t], t2_sb, h_plain[t][:], first, count)

        project_val(0)
        project_val(1)
        w2_front = cast_pair([nc.vector.tensor_copy, nc.scalar.copy], w2_raw, 0, "w2")
        first_tap(0)
        first_tap(1)
        quantize(w2_mx, 0, w2_front[:])
        for t in (2, 3):
            project_val(t)
            first_tap(t)
        w2_back = cast_pair([nc.scalar.copy], w2_raw, 1, "w2")
        first_gate(0)
        copy_h(0, 0, S)
        first_gate(1)
        copy_h(1, 0, S)
        quantize(w2_mx, 2 * P, w2_back[:])
        second_tap(0, 0, S)
        first_gate(2)
        first_gate(3)
        w1_grouped = keep.tile([P, H * PACK], BF16, name="w1_grouped", align_bytes=64)
        for pair in range(2):
            nc.scalar.copy(
                out=w1_grouped[:].rearrange("p (u t m j) -> p u m j t", u=2, t=2, j=PACK)[:, pair],
                in_=w1_raw[:].rearrange("p j (m u t) -> p u m j t", u=2, t=2)[:, pair],
            )
        second_tap(1, 0, S)
        quantize(w1_mx, 0, w1_grouped[:])
        copy_h(2, 0, S)
        y = []
        for c in range(CHUNKS):
            bank = psum.tile([P, PACK, CHUNK], F32, name="y%d" % c, tag="y%d" % c)
            for t in range(PACK):
                product(bank[:, t, :], w1_mx, plane_cols(t), x_mx, slice(c * CHUNK, (c + 1) * CHUNK))
            y.append(bank)
        w4_grouped = keep.tile([P, N * PACK], BF16, name="w4_grouped", align_bytes=64)
        nc.scalar.copy(
            out=w4_grouped[:].rearrange("p (c i j) -> p c j i", i=4, j=PACK),
            in_=w4_raw[:].rearrange("p j (c i) -> p c j i", i=4),
        )
        second_tap(2, 0, S)
        quantize(w4_mx, 0, w4_grouped[:])
        for first in (0, HALF):
            copy_h(last, first, HALF)

        out_rows = out.rearrange("(a p) s -> p a s", p=P)
        z_grouped = {}

        def second_gate(c):
            cols = slice(c * CHUNK, (c + 1) * CHUNK)
            z_grouped[c] = keep.tile([P, CHUNK * PACK], BF16, name="z_grouped%d" % c, align_bytes=64)
            nc.vector.tensor_tensor(
                z_grouped[c][:].rearrange("p (c i t) -> p c t i", i=2, t=PACK),
                h_sum[:, :, cols].rearrange("p t (c i) -> p c t i", i=2),
                y[c][:].rearrange("p t (c i) -> p c t i", i=2),
                MULT,
            )

        def last_layer(c):
            z_mx = mx_tiles("z%d" % c, CHUNK)
            quantize(z_mx, 0, z_grouped[c][:])
            cols = slice(c * CHUNK, (c + 1) * CHUNK)
            if c < 2:
                parts = [(0, N // P, nc.scalar.copy, nc.sync)]
            else:
                parts = [(0, 2, nc.scalar.copy, nc.scalar), (2, 2, nc.vector.tensor_copy, nc.sync)]
            for first, count, copy, queue in parts:
                acc = psum.tile([P, count, CHUNK], F32, name="acc", tag=("val_out", "e_out")[(c + first // 2) % 2], bufs=2)
                for a in range(count):
                    product(acc[:, a, :], w4_mx, plane_cols(first + a), z_mx, slice(0, CHUNK))
                result = keep.tile([P, count, CHUNK], F32, name="result%d_%d" % (c, first))
                copy(out=result[:], in_=acc[:])
                queue.dma_start(out=out_rows[:, first : first + count, cols], in_=result[:])

        second_tap(last, 0, HALF)
        for c in range(CHUNKS):
            if c < 2:
                second_tap(last, HALF + c * CHUNK, CHUNK)
            second_gate(c)
            if c >= 1:
                last_layer(c - 1)
        last_layer(CHUNKS - 1)
